import numpy as np
import ml_dtypes


def mxq(x, axis, fmt="e4m3"):
    dtype, down = {"e4m3": (ml_dtypes.float8_e4m3fn, 7), "e5m2": (ml_dtypes.float8_e5m2, 14)}[fmt]
    v = np.moveaxis(np.asarray(x, np.float32).astype(ml_dtypes.bfloat16).astype(np.float64), axis, -1)
    blocks = v.reshape(v.shape[:-1] + (-1, 32))
    amax = np.abs(blocks).max(-1, keepdims=True)
    byte = np.maximum(np.where(amax > 0, np.frexp(amax)[1] - 1 + 127, 0) - down, 1)
    scale = np.exp2(byte - 127.0)
    codes = (blocks / scale).astype(np.float32).astype(dtype).astype(np.float64)
    return np.moveaxis((codes * scale).reshape(v.shape), -1, axis)


WIDE = False


def mx_kscale(k):
    if not WIDE:
        return np.ones(k)
    levels = np.array([10, -10, 5, -5, 0])
    if k % 512:
        return np.exp2(np.random.permutation(np.resize(levels, k // 32))).repeat(32)
    a = np.empty((k // 512, 16))
    for p in range(k // 512):
        a[p, :8] = np.random.permutation(np.resize(levels, 8))
        for g in range(8):
            far = levels[np.abs(levels - a[p, g]) >= 10]
            a[p, g + 8] = far[np.random.randint(len(far))]
    return np.exp2(a.ravel()).repeat(32)


def f64(x):
    return np.asarray(x).astype(np.float64)


def striped(idx):
    return np.tile(np.asarray(idx).reshape(-1, 16).T, (8, 1)).astype(np.uint16)


def unstriped(offs):
    return offs[:16].T.reshape(-1).astype(np.int64)


E2M1 = np.array([0.0, 0.5, 1.0, 1.5, 2.0, 3.0, 4.0, 6.0, -0.0, -0.5, -1.0, -1.5, -2.0, -3.0, -4.0, -6.0])


def pack_weight(w, fmt):
    k, n = w.shape
    w = f64(np.asarray(w, np.float32).astype(ml_dtypes.bfloat16)).reshape(k // 32, 32, n)
    amax = np.abs(w).max(1)
    if fmt == "e4m3":
        byte = np.frexp(amax)[1] - 1 + 127 - 7
    else:
        mant, ex = np.frexp(amax / 6.0)
        byte = np.where(mant > 0.5, ex, ex - 1) + 127
    byte = np.clip(np.where(amax > 0, byte, 1), 1, 254)
    scaled = (w * np.exp2(127.0 - byte)[:, None, :]).reshape(k, n).astype(np.float32)
    by_word = np.ascontiguousarray(scaled.reshape(k // 512, 128, 4, n).transpose(0, 1, 3, 2))
    if fmt == "e4m3":
        words = by_word.astype(ml_dtypes.float8_e4m3fn).view(np.uint8)
    else:
        c = by_word.astype(ml_dtypes.float4_e2m1fn).view(np.uint8) & 0xF
        words = (c[..., 0::2] | (c[..., 1::2] << 4)).reshape(k // 512, 128, 2 * n)
    return np.ascontiguousarray(words), np.ascontiguousarray(byte.astype(np.uint8).reshape(k // 512, 16, n))


def unpack_weight(words, scales, fmt):
    g, _, n = scales.shape
    words = np.ascontiguousarray(words).reshape(g, 128, n, -1)
    if fmt == "e4m3":
        vals = words.view(ml_dtypes.float8_e4m3fn).astype(np.float64)
    else:
        nib = np.empty((g, 128, n, 4), np.uint8)
        nib[..., 0::2] = words & 0xF
        nib[..., 1::2] = words >> 4
        vals = E2M1[nib]
    vals = vals * np.repeat(np.exp2(scales.astype(np.float64) - 127.0), 8, axis=1)[..., None]
    return vals.transpose(0, 1, 3, 2).reshape(g * 512, n)


def sigmoid(v):
    return 1.0 / (1.0 + np.exp(-v))


D, E, T, I, Q, G = 512, 512, 2048, 512, 128, 32


def setup_inputs():
    n = np.random.standard_normal
    idx = np.random.permutation(T)[:I]
    fd = mx_kscale(D)
    fi = mx_kscale(I)
    ti = np.ones(T)
    ti[idx] = fi
    keysp = pack_weight(n((D, T)) / fd[:, None], "e4m3")
    return {
        "query": (n((D, Q)) * 0.8 / np.sqrt(D) * fd[:, None]).astype(np.float32),
        "keys_words": keysp[0],
        "keys_scales": keysp[1],
        "th": (np.random.uniform(-0.5, 0.5, (Q, 1))).astype(np.float32),
        "sharp": (np.random.uniform(1.0, 3.0, (Q, 1))).astype(np.float32),
        "os": (np.random.uniform(0.5, 2.0, (1, I)) * fi).astype(np.float32),
        "vals": (n((E, T)) / ti).astype(np.float32),
        "offs": striped(idx),
    }


def reference(query, keys_words, keys_scales, th, sharp, os, vals, offs):
    idx = unstriped(offs)
    keysu = unpack_weight(keys_words, keys_scales, "e4m3")
    queryq = mxq(f64(query), 0, "e4m3")
    keysidxg = keysu[:, idx]
    a = queryq.T @ keysidxg
    s = a.reshape(Q, G, I // G).mean(axis=2) * f64(sharp)
    p = np.exp(s - np.max(s, axis=1, keepdims=True))
    z = np.sum(p, axis=1, keepdims=True)
    r = p / z
    rr = np.repeat(r, I // G, axis=1)
    w = rr * sigmoid(a - f64(th))
    wo1 = w * f64(os)
    wt1 = wo1.T
    vt1 = f64(vals)[:, idx].T
    wt1q = mxq(wt1, 0, "e4m3")
    vt1q = mxq(vt1, 0, "e4m3")
    o = wt1q.T @ vt1q
    return o

@@ -1,0 +1,174 @@
+from contextlib import ExitStack
+
+import concourse.mybir as mybir
+from concourse.masks import make_identity
+
+D, E, T, I, Q, G = 512, 512, 2048, 512, 128, 32
+FLOPS = 2 * Q * I * (D + E)
+
+F32 = mybir.dt.float32
+BF16 = mybir.dt.bfloat16
+I32 = mybir.dt.int32
+U32 = mybir.dt.uint32
+U16 = mybir.dt.uint16
+U8 = mybir.dt.uint8
+FP8X4 = mybir.dt.float8_e4m3fn_x4
+ALU = mybir.AluOpType
+ACT = mybir.ActivationFunctionType
+
+P = 128
+PACK = 4
+PAGE = I // G
+E_TILES = E // P
+VAL_SLOTS = ("slot_v", "slot_a", "slot_c", "slot_b")
+PICK_SLOTS = ("slot_d", "slot_e", "slot_f", "slot_g")
+
+
+def tile_attend_pagetimessigmoid_kernel(tc, query, keys_words, keys_scales, th, sharp, slot_factor, vals, offs, out):
+    nc = tc.nc
+    with ExitStack() as ctx:
+        sb = ctx.enter_context(tc.tile_pool(name="sb", bufs=1))
+        ps = ctx.enter_context(tc.psum_pool(name="ps", bufs=1))
+
+        offsets = sb.tile([P, I // 16], U16, name="offsets")
+        key_scale_pool = sb.tile([P, T], U8, name="key_scale_pool", tag="slot_b", align_bytes=64)
+        key_word_pool = sb.tile([P, T], I32, name="key_word_pool", tag="slot_c", align_bytes=64)
+        query_raw = sb.tile([P, PACK, Q], F32, name="query_raw", tag="slot_a", align_bytes=64)
+        th_col = sb.tile([P, 1], F32, name="th_col")
+        sharp_col = sb.tile([P, 1], F32, name="sharp_col")
+        os_cols = sb.tile([P, PACK], F32, name="os_cols")
+        ident = sb.tile([P, P], F32, name="ident")
+
+        nc.vector.memset(key_scale_pool[:].bitcast(I32), 0)
+        nc.sync.dma_start(offsets[:], offs)
+        nc.sync.dma_start(out=query_raw[:], in_=query.rearrange("(p t) q -> p t q", t=PACK))
+        nc.sync.dma_start(out=key_word_pool[:], in_=keys_words[0].rearrange("p n t -> p (n t)").bitcast(I32))
+        for quad in range(4):
+            nc.scalar.dma_start(
+                out=key_scale_pool[32 * quad : 32 * quad + 4, :].bitcast(I32),
+                in_=keys_scales[0, 4 * quad : 4 * quad + 4, :].bitcast(I32),
+            )
+        nc.gpsimd.dma_start(out=th_col[:], in_=th)
+        nc.gpsimd.dma_start(out=sharp_col[:], in_=sharp)
+        make_identity(nc, ident[:])
+        nc.gpsimd.dma_start(out=os_cols[:], in_=slot_factor.rearrange("o (p t) -> p (o t)", t=PACK))
+
+        warm = sb.tile([P, 2], F32, name="warm")
+        nc.vector.memset(warm[:, 0:1], 0.0)
+        nc.scalar.activation(warm[:, 1:2], warm[:, 0:1], ACT.Sigmoid)
+
+        query_bf = sb.tile([P, Q, PACK], BF16, name="query_bf", align_bytes=64)
+        nc.vector.tensor_copy(out=query_bf[:], in_=query_raw[:].rearrange("p t q -> p q t"))
+        query_codes = sb.tile([P, Q], U32, name="query_codes", align_bytes=64)
+        query_scales = sb.tile([P, Q], U8, name="query_scales", align_bytes=64)
+        nc.vector.quantize_mx(
+            out=query_codes[:].bitcast(FP8X4), scales=query_scales[:], in_=query_bf[:].rearrange("p q t -> p (q t)")
+        )
+        neg_th = sb.tile([P, 1], F32, name="neg_th")
+        nc.gpsimd.tensor_scalar(neg_th[:], th_col[:], -1.0, 0.0, ALU.mult, ALU.add)
+        neg_sharp = sb.tile([P, 1], F32, name="neg_sharp")
+        nc.gpsimd.tensor_scalar(neg_sharp[:], sharp_col[:], -1.0 / PAGE, 0.0, ALU.mult, ALU.add)
+
+        key_scales = sb.tile([P, I], U8, name="key_scales", align_bytes=64)
+        nc.vector.tensor_copy(key_scales[:], key_scale_pool[:].indirect(offsets[:]))
+        page_sums = sb.tile([P, G], F32, name="page_sums", tag="slot_d", align_bytes=64)
+        gate = sb.tile([P, PACK, P], F32, name="gate")
+        half = I // 2
+        scores = []
+        key_codes = sb.tile([P, I], U32, name="key_codes", tag="slot_b", align_bytes=64)
+        for h in range(2):
+            nc.vector.tensor_copy(
+                key_codes[:, h * half : (h + 1) * half], key_word_pool[:].bitcast(U32).indirect(offsets[:, h * half // 16 : (h + 1) * half // 16])
+            )
+            bank = ps.tile([P, half], F32, name="scores%d" % h)
+            nc.tensor.matmul_mx(
+                out=bank[:],
+                lhsT=query_codes[:].bitcast(FP8X4),
+                lhsT_scale=query_scales[:],
+                rhs=key_codes[:, h * half : (h + 1) * half].bitcast(FP8X4),
+                rhs_scale=key_scales[:, h * half : (h + 1) * half],
+                start=True,
+                stop=True,
+            )
+            scores.append(bank)
+        for h in range(2):
+            nc.scalar.activation(
+                gate[:, :, h * P // 2 : (h + 1) * P // 2],
+                scores[h][:].rearrange("q (p t) -> q t p", t=PACK),
+                ACT.Sigmoid,
+                bias=neg_th[:],
+            )
+            nc.vector.tensor_reduce(
+                page_sums[:, h * G // 2 : (h + 1) * G // 2],
+                scores[h][:].rearrange("q (g j) -> q g j", j=PAGE),
+                mybir.AxisListType.X,
+                ALU.add,
+            )
+        neg_s = sb.tile([P, G], F32, name="neg_s")
+        neg_max = sb.tile([P, 1], F32, name="neg_max")
+        nc.vector.tensor_scalar(neg_s[:], page_sums[:], neg_sharp[:], None, ALU.mult, ALU.min, accum_out=neg_max[:])
+        page_exp = sb.tile([P, G], F32, name="page_exp", tag="slot_e", align_bytes=64)
+        exp_sum = sb.tile([P, 1], F32, name="exp_sum")
+        nc.scalar.activation(page_exp[:], neg_s[:], ACT.Exp, bias=neg_max[:], scale=-1.0, accum_out=exp_sum[:])
+        inv_sum = sb.tile([P, 1], F32, name="inv_sum")
+        nc.vector.reciprocal(inv_sum[:], exp_sum[:])
+        share = sb.tile([P, G, P // G], F32, name="share")
+        nc.vector.tensor_scalar(
+            share[:],
+            page_exp[:].rearrange("q (g b) -> q g b", b=1).to_broadcast([P, G, P // G]),
+            inv_sum[:],
+            None,
+            ALU.mult,
+        )
+        share_t = ps.tile([P, Q], F32, name="share_t")
+        nc.tensor.transpose(share_t[:], share[:].rearrange("q g b -> q (g b)"), ident[:])
+        gate_t = ps.tile([P, PACK, Q], F32, name="gate_t")
+        for t in range(PACK):
+            nc.tensor.transpose(gate_t[:, t, :], gate[:, t, :], ident[:])
+        gate_os = sb.tile([P, PACK, Q], F32, name="gate_os")
+        for t in range(PACK):
+            nc.scalar.activation(gate_os[:, t, :], gate_t[:, t, :], ACT.Copy, scale=os_cols[:, t : t + 1])
+        weights_bf = sb.tile([P, Q, PACK], BF16, name="weights_bf", tag="slot_f", align_bytes=64)
+        nc.vector.tensor_tensor(
+            weights_bf[:],
+            gate_os[:].rearrange("p t q -> p q t"),
+            share_t[:].rearrange("p (q a) -> p q a", a=1).to_broadcast([P, Q, PACK]),
+            ALU.mult,
+        )
+        weight_codes = sb.tile([P, Q], U32, name="weight_codes", align_bytes=64)
+        weight_scales = sb.tile([P, Q], U8, name="weight_scales", align_bytes=64)
+        nc.vector.quantize_mx(
+            out=weight_codes[:].bitcast(FP8X4),
+            scales=weight_scales[:],
+            in_=weights_bf[:].rearrange("p q t -> p (q t)"),
+        )
+
+        for j in range(E_TILES):
+            val_pool = sb.tile([P, T], F32, name="val_pool%d" % j, tag=VAL_SLOTS[j], align_bytes=64)
+            nc.sync.dma_start(out=val_pool[:], in_=vals[j * P : (j + 1) * P, :])
+            picked = sb.tile([P, I], BF16, name="picked%d" % j, tag=PICK_SLOTS[j], align_bytes=64)
+            nc.vector.tensor_copy(picked[:], val_pool[:].indirect(offsets[:]))
+            pairs = picked[:].bitcast(F32)
+            turned = ps.tile([P, 2, P], F32, name="turned", bufs=2)
+            for u in range(2):
+                nc.tensor.transpose(turned[:, u, :], pairs[:, u : I // 2 : 2], ident[:])
+            vals_bf = sb.tile([P, P, PACK], BF16, name="vals_bf%d" % j, align_bytes=64)
+            nc.scalar.copy(vals_bf[:].bitcast(F32), turned[:].rearrange("p u e -> p e u"))
+            val_codes = sb.tile([P, P], U32, name="val_codes%d" % j, align_bytes=64)
+            val_scales = sb.tile([P, P], U8, name="val_scales%d" % j, align_bytes=64)
+            nc.vector.quantize_mx(
+                out=val_codes[:].bitcast(FP8X4), scales=val_scales[:], in_=vals_bf[:].rearrange("p e t -> p (e t)")
+            )
+            acc = ps.tile([Q, P], F32, name="acc", bufs=2)
+            nc.tensor.matmul_mx(
+                out=acc[:],
+                lhsT=weight_codes[:].bitcast(FP8X4),
+                lhsT_scale=weight_scales[:],
+                rhs=val_codes[:].bitcast(FP8X4),
+                rhs_scale=val_scales[:],
+                start=True,
+                stop=True,
+            )
+            result = sb.tile([Q, P], F32, name="result%d" % j)
+            nc.scalar.copy(result[:], acc[:])
+            nc.sync.dma_start(out=out[:, j * P : (j + 1) * P], in_=result[:])

@@ -20,8 +20,8 @@ P = 128
 PACK = 4
 PAGE = I // G
 E_TILES = E // P
-VAL_SLOTS = ("slot_v", "slot_a", "slot_c", "slot_b")
-PICK_SLOTS = ("slot_d", "slot_e", "slot_f", "slot_g")
+VAL_SLOTS = ("slot_v", "slot_a", "slot_b", "slot_c")
+PICK_SLOTS = ("slot_h", "slot_f", "slot_g", "slot_i")
 
 
 def tile_attend_pagetimessigmoid_kernel(tc, query, keys_words, keys_scales, th, sharp, slot_factor, vals, offs, out):
@@ -31,7 +31,7 @@ def tile_attend_pagetimessigmoid_kernel(tc, query, keys_words, keys_scales, th, 
         ps = ctx.enter_context(tc.psum_pool(name="ps", bufs=1))
 
         offsets = sb.tile([P, I // 16], U16, name="offsets")
-        key_scale_pool = sb.tile([P, T], U8, name="key_scale_pool", tag="slot_b", align_bytes=64)
+        key_scale_pool = sb.tile([P, T], U8, name="key_scale_pool", align_bytes=64)
         key_word_pool = sb.tile([P, T], I32, name="key_word_pool", tag="slot_c", align_bytes=64)
         query_raw = sb.tile([P, PACK, Q], F32, name="query_raw", tag="slot_a", align_bytes=64)
         th_col = sb.tile([P, 1], F32, name="th_col")
@@ -48,16 +48,16 @@ def tile_attend_pagetimessigmoid_kernel(tc, query, keys_words, keys_scales, th, 
                 out=key_scale_pool[32 * quad : 32 * quad + 4, :].bitcast(I32),
                 in_=keys_scales[0, 4 * quad : 4 * quad + 4, :].bitcast(I32),
             )
-        nc.gpsimd.dma_start(out=th_col[:], in_=th)
-        nc.gpsimd.dma_start(out=sharp_col[:], in_=sharp)
+        nc.scalar.dma_start(out=th_col[:], in_=th)
+        nc.scalar.dma_start(out=sharp_col[:], in_=sharp)
         make_identity(nc, ident[:])
-        nc.gpsimd.dma_start(out=os_cols[:], in_=slot_factor.rearrange("o (p t) -> p (o t)", t=PACK))
+        nc.scalar.dma_start(out=os_cols[:], in_=slot_factor.rearrange("o (p t) -> p (o t)", t=PACK))
 
         warm = sb.tile([P, 2], F32, name="warm")
         nc.vector.memset(warm[:, 0:1], 0.0)
         nc.scalar.activation(warm[:, 1:2], warm[:, 0:1], ACT.Sigmoid)
 
-        query_bf = sb.tile([P, Q, PACK], BF16, name="query_bf", align_bytes=64)
+        query_bf = sb.tile([P, Q, PACK], BF16, name="query_bf", tag="slot_b", align_bytes=64)
         nc.vector.tensor_copy(out=query_bf[:], in_=query_raw[:].rearrange("p t q -> p q t"))
         query_codes = sb.tile([P, Q], U32, name="query_codes", align_bytes=64)
         query_scales = sb.tile([P, Q], U8, name="query_scales", align_bytes=64)
@@ -70,15 +70,16 @@ def tile_attend_pagetimessigmoid_kernel(tc, query, keys_words, keys_scales, th, 
         nc.gpsimd.tensor_scalar(neg_sharp[:], sharp_col[:], -1.0 / PAGE, 0.0, ALU.mult, ALU.add)
 
         key_scales = sb.tile([P, I], U8, name="key_scales", align_bytes=64)
-        nc.vector.tensor_copy(key_scales[:], key_scale_pool[:].indirect(offsets[:]))
-        page_sums = sb.tile([P, G], F32, name="page_sums", tag="slot_d", align_bytes=64)
+        page_sums = sb.tile([P, G], F32, name="page_sums", tag="slot_f", align_bytes=64)
         gate = sb.tile([P, PACK, P], F32, name="gate")
+        key_codes = sb.tile([P, I], U32, name="key_codes", align_bytes=64)
+        nc.vector.tensor_copy(key_codes[:], key_word_pool[:].bitcast(U32).indirect(offsets[:]))
         half = I // 2
         scores = []
-        key_codes = sb.tile([P, I], U32, name="key_codes", tag="slot_b", align_bytes=64)
         for h in range(2):
             nc.vector.tensor_copy(
-                key_codes[:, h * half : (h + 1) * half], key_word_pool[:].bitcast(U32).indirect(offsets[:, h * half // 16 : (h + 1) * half // 16])
+                key_scales[:, h * half : (h + 1) * half],
+                key_scale_pool[:].indirect(offsets[:, h * half // 16 : (h + 1) * half // 16]),
             )
             bank = ps.tile([P, half], F32, name="scores%d" % h)
             nc.tensor.matmul_mx(
@@ -90,59 +91,47 @@ def tile_attend_pagetimessigmoid_kernel(tc, query, keys_words, keys_scales, th, 
                 start=True,
                 stop=True,
             )
-            scores.append(bank)
-        for h in range(2):
             nc.scalar.activation(
                 gate[:, :, h * P // 2 : (h + 1) * P // 2],
-                scores[h][:].rearrange("q (p t) -> q t p", t=PACK),
+                bank[:].rearrange("q (p t) -> q t p", t=PACK),
                 ACT.Sigmoid,
                 bias=neg_th[:],
             )
+            scores.append(bank)
+        warm_exp = sb.tile([P, 1], F32, name="warm_exp")
+        nc.scalar.activation(warm_exp[:], gate[:, 0, P - 1 : P], ACT.Exp)
+        for h in range(2):
             nc.vector.tensor_reduce(
                 page_sums[:, h * G // 2 : (h + 1) * G // 2],
                 scores[h][:].rearrange("q (g j) -> q g j", j=PAGE),
                 mybir.AxisListType.X,
                 ALU.add,
             )
-        neg_s = sb.tile([P, G], F32, name="neg_s")
-        neg_max = sb.tile([P, 1], F32, name="neg_max")
+        neg_s = sb.tile([P, G], F32, name="neg_s", tag="slot_d", align_bytes=64)
+        neg_max = sb.tile([P, 1], F32, name="neg_max", tag="slot_e", align_bytes=64)
         nc.vector.tensor_scalar(neg_s[:], page_sums[:], neg_sharp[:], None, ALU.mult, ALU.min, accum_out=neg_max[:])
-        page_exp = sb.tile([P, G], F32, name="page_exp", tag="slot_e", align_bytes=64)
-        exp_sum = sb.tile([P, 1], F32, name="exp_sum")
+        page_exp = sb.tile([P, G], F32, name="page_exp")
+        exp_sum = sb.tile([P, 1], F32, name="exp_sum", tag="slot_g", align_bytes=64)
         nc.scalar.activation(page_exp[:], neg_s[:], ACT.Exp, bias=neg_max[:], scale=-1.0, accum_out=exp_sum[:])
         inv_sum = sb.tile([P, 1], F32, name="inv_sum")
         nc.vector.reciprocal(inv_sum[:], exp_sum[:])
         share = sb.tile([P, G, P // G], F32, name="share")
-        nc.vector.tensor_scalar(
+        nc.scalar.activation(
             share[:],
             page_exp[:].rearrange("q (g b) -> q g b", b=1).to_broadcast([P, G, P // G]),
-            inv_sum[:],
-            None,
-            ALU.mult,
+            ACT.Copy,
+            scale=inv_sum[:],
         )
         share_t = ps.tile([P, Q], F32, name="share_t")
         nc.tensor.transpose(share_t[:], share[:].rearrange("q g b -> q (g b)"), ident[:])
         gate_t = ps.tile([P, PACK, Q], F32, name="gate_t")
         for t in range(PACK):
             nc.tensor.transpose(gate_t[:, t, :], gate[:, t, :], ident[:])
-        gate_os = sb.tile([P, PACK, Q], F32, name="gate_os")
+        gate_os = sb.tile([P, PACK, Q], F32, name="gate_os", tag="slot_e", align_bytes=64)
         for t in range(PACK):
             nc.scalar.activation(gate_os[:, t, :], gate_t[:, t, :], ACT.Copy, scale=os_cols[:, t : t + 1])
-        weights_bf = sb.tile([P, Q, PACK], BF16, name="weights_bf", tag="slot_f", align_bytes=64)
-        nc.vector.tensor_tensor(
-            weights_bf[:],
-            gate_os[:].rearrange("p t q -> p q t"),
-            share_t[:].rearrange("p (q a) -> p q a", a=1).to_broadcast([P, Q, PACK]),
-            ALU.mult,
-        )
-        weight_codes = sb.tile([P, Q], U32, name="weight_codes", align_bytes=64)
-        weight_scales = sb.tile([P, Q], U8, name="weight_scales", align_bytes=64)
-        nc.vector.quantize_mx(
-            out=weight_codes[:].bitcast(FP8X4),
-            scales=weight_scales[:],
-            in_=weights_bf[:].rearrange("p q t -> p (q t)"),
-        )
-
+        first_bf = sb.tile([P, 2 * I], BF16, name="first_bf", tag="slot_d", align_bytes=64)
+        last_bf = sb.tile([P, P * PACK], BF16, name="last_bf", align_bytes=64)
         for j in range(E_TILES):
             val_pool = sb.tile([P, T], F32, name="val_pool%d" % j, tag=VAL_SLOTS[j], align_bytes=64)
             nc.sync.dma_start(out=val_pool[:], in_=vals[j * P : (j + 1) * P, :])
@@ -152,23 +141,54 @@ def tile_attend_pagetimessigmoid_kernel(tc, query, keys_words, keys_scales, th, 
             turned = ps.tile([P, 2, P], F32, name="turned", bufs=2)
             for u in range(2):
                 nc.tensor.transpose(turned[:, u, :], pairs[:, u : I // 2 : 2], ident[:])
-            vals_bf = sb.tile([P, P, PACK], BF16, name="vals_bf%d" % j, align_bytes=64)
-            nc.scalar.copy(vals_bf[:].bitcast(F32), turned[:].rearrange("p u e -> p e u"))
-            val_codes = sb.tile([P, P], U32, name="val_codes%d" % j, align_bytes=64)
-            val_scales = sb.tile([P, P], U8, name="val_scales%d" % j, align_bytes=64)
-            nc.vector.quantize_mx(
-                out=val_codes[:].bitcast(FP8X4), scales=val_scales[:], in_=vals_bf[:].rearrange("p e t -> p (e t)")
+            if j == 2:
+                mixed_bf = sb.tile([P, 2 * I], BF16, name="mixed_bf", tag="slot_b", align_bytes=64)
+                nc.vector.tensor_tensor(
+                    mixed_bf[:, :I].rearrange("p (q t) -> p q t", t=PACK),
+                    gate_os[:].rearrange("p t q -> p q t"),
+                    share_t[:].rearrange("p (q a) -> p q a", a=1).to_broadcast([P, Q, PACK]),
+                    ALU.mult,
+                )
+                vals_bf = mixed_bf[:, I:]
+            elif j == 3:
+                vals_bf = last_bf[:]
+            else:
+                vals_bf = first_bf[:, j * I : (j + 1) * I]
+            nc.scalar.copy(
+                vals_bf.bitcast(F32).rearrange("p (e u) -> p e u", u=2), turned[:].rearrange("p u e -> p e u")
             )
-            acc = ps.tile([Q, P], F32, name="acc", bufs=2)
+
+        early_codes = sb.tile([P, E_TILES * P], U32, name="early_codes", tag="slot_c", align_bytes=64)
+        early_scales = sb.tile([P, E_TILES * P], U8, name="early_scales", align_bytes=64)
+        nc.vector.quantize_mx(
+            out=early_codes[:, : 2 * P].bitcast(FP8X4), scales=early_scales[:, : 2 * P], in_=mixed_bf[:]
+        )
+        nc.vector.quantize_mx(
+            out=early_codes[:, 2 * P :].bitcast(FP8X4), scales=early_scales[:, 2 * P :], in_=first_bf[:]
+        )
+        last_codes = sb.tile([P, P], U32, name="last_codes", align_bytes=64)
+        last_scales = sb.tile([P, P], U8, name="last_scales", align_bytes=64)
+        nc.vector.quantize_mx(out=last_codes[:].bitcast(FP8X4), scales=last_scales[:], in_=last_bf[:])
+
+        acc_early = ps.tile([Q, E - P], F32, name="acc_early")
+        acc_last = ps.tile([Q, P], F32, name="acc_last")
+        for acc, codes, scales in (
+            (acc_early[:, 2 * P :], early_codes[:, Q : Q + P], early_scales[:, Q : Q + P]),
+            (acc_early[:, : 2 * P], early_codes[:, Q + P :], early_scales[:, Q + P :]),
+            (acc_last[:], last_codes[:], last_scales[:]),
+        ):
             nc.tensor.matmul_mx(
-                out=acc[:],
-                lhsT=weight_codes[:].bitcast(FP8X4),
-                lhsT_scale=weight_scales[:],
-                rhs=val_codes[:].bitcast(FP8X4),
-                rhs_scale=val_scales[:],
+                out=acc,
+                lhsT=early_codes[:, :Q].bitcast(FP8X4),
+                lhsT_scale=early_scales[:, :Q],
+                rhs=codes.bitcast(FP8X4),
+                rhs_scale=scales,
                 start=True,
                 stop=True,
             )
-            result = sb.tile([Q, P], F32, name="result%d" % j)
-            nc.scalar.copy(result[:], acc[:])
-            nc.sync.dma_start(out=out[:, j * P : (j + 1) * P], in_=result[:])
+        result_early = sb.tile([Q, E - P], F32, name="result_early")
+        nc.scalar.copy(result_early[:], acc_early[:])
+        nc.sync.dma_start(out=out[:, : E - P], in_=result_early[:])
+        result_last = sb.tile([Q, P], F32, name="result_last")
+        nc.vector.tensor_copy(result_last[:], acc_last[:])
+        nc.sync.dma_start(out=out[:, E - P :], in_=result_last[:])

@@ -40,8 +40,8 @@ def tile_attend_pagetimessigmoid_kernel(tc, query, keys_words, keys_scales, th, 
         ident = sb.tile([P, P], F32, name="ident")
 
         nc.vector.memset(key_scale_pool[:].bitcast(I32), 0)
-        nc.sync.dma_start(offsets[:], offs)
         nc.sync.dma_start(out=query_raw[:], in_=query.rearrange("(p t) q -> p t q", t=PACK))
+        nc.sync.dma_start(offsets[:], offs)
         nc.sync.dma_start(out=key_word_pool[:], in_=keys_words[0].rearrange("p n t -> p (n t)").bitcast(I32))
         for quad in range(4):
             nc.scalar.dma_start(
@@ -154,7 +154,8 @@ def tile_attend_pagetimessigmoid_kernel(tc, query, keys_words, keys_scales, th, 
                 vals_bf = last_bf[:]
             else:
                 vals_bf = first_bf[:, j * I : (j + 1) * I]
-            nc.scalar.copy(
+            copy_out = nc.vector.tensor_copy if j == 3 else nc.scalar.copy
+            copy_out(
                 vals_bf.bitcast(F32).rearrange("p (e u) -> p e u", u=2), turned[:].rearrange("p u e -> p e u")
             )
 
@@ -190,5 +191,5 @@ def tile_attend_pagetimessigmoid_kernel(tc, query, keys_words, keys_scales, th, 
         nc.scalar.copy(result_early[:], acc_early[:])
         nc.sync.dma_start(out=out[:, : E - P], in_=result_early[:])
         result_last = sb.tile([Q, P], F32, name="result_last")
-        nc.vector.tensor_copy(result_last[:], acc_last[:])
-        nc.sync.dma_start(out=out[:, E - P :], in_=result_last[:])
+        nc.scalar.copy(result_last[:], acc_last[:])
+        nc.scalar.dma_start(out=out[:, E - P :], in_=result_last[:])

from contextlib import ExitStack

import concourse.mybir as mybir
from concourse.masks import make_identity

D, E, T, I, Q, G = 512, 512, 2048, 512, 128, 32
FLOPS = 2 * Q * I * (D + E)

F32 = mybir.dt.float32
BF16 = mybir.dt.bfloat16
I32 = mybir.dt.int32
U32 = mybir.dt.uint32
U16 = mybir.dt.uint16
U8 = mybir.dt.uint8
FP8X4 = mybir.dt.float8_e4m3fn_x4
ALU = mybir.AluOpType
ACT = mybir.ActivationFunctionType

P = 128
PACK = 4
PAGE = I // G
E_TILES = E // P
VAL_SLOTS = ("slot_v", "slot_a", "slot_b", "slot_c")
PICK_SLOTS = ("slot_h", "slot_f", "slot_g", "slot_i")


def tile_attend_pagetimessigmoid_kernel(tc, query, keys_words, keys_scales, th, sharp, slot_factor, vals, offs, out):
    nc = tc.nc
    with ExitStack() as ctx:
        sb = ctx.enter_context(tc.tile_pool(name="sb", bufs=1))
        ps = ctx.enter_context(tc.psum_pool(name="ps", bufs=1))

        offsets = sb.tile([P, I // 16], U16, name="offsets")
        key_scale_pool = sb.tile([P, T], U8, name="key_scale_pool", align_bytes=64)
        key_word_pool = sb.tile([P, T], I32, name="key_word_pool", tag="slot_c", align_bytes=64)
        query_raw = sb.tile([P, PACK, Q], F32, name="query_raw", tag="slot_a", align_bytes=64)
        th_col = sb.tile([P, 1], F32, name="th_col")
        sharp_col = sb.tile([P, 1], F32, name="sharp_col")
        os_cols = sb.tile([P, PACK], F32, name="os_cols")
        ident = sb.tile([P, P], F32, name="ident")

        nc.vector.memset(key_scale_pool[:].bitcast(I32), 0)
        nc.sync.dma_start(out=query_raw[:], in_=query.rearrange("(p t) q -> p t q", t=PACK))
        nc.sync.dma_start(offsets[:], offs)
        nc.sync.dma_start(out=key_word_pool[:], in_=keys_words[0].rearrange("p n t -> p (n t)").bitcast(I32))
        for quad in range(4):
            nc.scalar.dma_start(
                out=key_scale_pool[32 * quad : 32 * quad + 4, :].bitcast(I32),
                in_=keys_scales[0, 4 * quad : 4 * quad + 4, :].bitcast(I32),
            )
        nc.scalar.dma_start(out=th_col[:], in_=th)
        nc.scalar.dma_start(out=sharp_col[:], in_=sharp)
        make_identity(nc, ident[:])
        nc.scalar.dma_start(out=os_cols[:], in_=slot_factor.rearrange("o (p t) -> p (o t)", t=PACK))

        warm = sb.tile([P, 2], F32, name="warm")
        nc.vector.memset(warm[:, 0:1], 0.0)
        nc.scalar.activation(warm[:, 1:2], warm[:, 0:1], ACT.Sigmoid)

        query_bf = sb.tile([P, Q, PACK], BF16, name="query_bf", tag="slot_b", align_bytes=64)
        nc.vector.tensor_copy(out=query_bf[:], in_=query_raw[:].rearrange("p t q -> p q t"))
        query_codes = sb.tile([P, Q], U32, name="query_codes", align_bytes=64)
        query_scales = sb.tile([P, Q], U8, name="query_scales", align_bytes=64)
        nc.vector.quantize_mx(
            out=query_codes[:].bitcast(FP8X4), scales=query_scales[:], in_=query_bf[:].rearrange("p q t -> p (q t)")
        )
        neg_th = sb.tile([P, 1], F32, name="neg_th")
        nc.gpsimd.tensor_scalar(neg_th[:], th_col[:], -1.0, 0.0, ALU.mult, ALU.add)
        neg_sharp = sb.tile([P, 1], F32, name="neg_sharp")
        nc.gpsimd.tensor_scalar(neg_sharp[:], sharp_col[:], -1.0 / PAGE, 0.0, ALU.mult, ALU.add)

        key_scales = sb.tile([P, I], U8, name="key_scales", align_bytes=64)
        page_sums = sb.tile([P, G], F32, name="page_sums", tag="slot_f", align_bytes=64)
        gate = sb.tile([P, PACK, P], F32, name="gate")
        key_codes = sb.tile([P, I], U32, name="key_codes", align_bytes=64)
        nc.vector.tensor_copy(key_codes[:], key_word_pool[:].bitcast(U32).indirect(offsets[:]))
        half = I // 2
        scores = []
        for h in range(2):
            nc.vector.tensor_copy(
                key_scales[:, h * half : (h + 1) * half],
                key_scale_pool[:].indirect(offsets[:, h * half // 16 : (h + 1) * half // 16]),
            )
            bank = ps.tile([P, half], F32, name="scores%d" % h)
            nc.tensor.matmul_mx(
                out=bank[:],
                lhsT=query_codes[:].bitcast(FP8X4),
                lhsT_scale=query_scales[:],
                rhs=key_codes[:, h * half : (h + 1) * half].bitcast(FP8X4),
                rhs_scale=key_scales[:, h * half : (h + 1) * half],
                start=True,
                stop=True,
            )
            nc.scalar.activation(
                gate[:, :, h * P // 2 : (h + 1) * P // 2],
                bank[:].rearrange("q (p t) -> q t p", t=PACK),
                ACT.Sigmoid,
                bias=neg_th[:],
            )
            scores.append(bank)
        warm_exp = sb.tile([P, 1], F32, name="warm_exp")
        nc.scalar.activation(warm_exp[:], gate[:, 0, P - 1 : P], ACT.Exp)
        for h in range(2):
            nc.vector.tensor_reduce(
                page_sums[:, h * G // 2 : (h + 1) * G // 2],
                scores[h][:].rearrange("q (g j) -> q g j", j=PAGE),
                mybir.AxisListType.X,
                ALU.add,
            )
        neg_s = sb.tile([P, G], F32, name="neg_s", tag="slot_d", align_bytes=64)
        neg_max = sb.tile([P, 1], F32, name="neg_max", tag="slot_e", align_bytes=64)
        nc.vector.tensor_scalar(neg_s[:], page_sums[:], neg_sharp[:], None, ALU.mult, ALU.min, accum_out=neg_max[:])
        page_exp = sb.tile([P, G], F32, name="page_exp")
        exp_sum = sb.tile([P, 1], F32, name="exp_sum", tag="slot_g", align_bytes=64)
        nc.scalar.activation(page_exp[:], neg_s[:], ACT.Exp, bias=neg_max[:], scale=-1.0, accum_out=exp_sum[:])
        inv_sum = sb.tile([P, 1], F32, name="inv_sum")
        nc.vector.reciprocal(inv_sum[:], exp_sum[:])
        share = sb.tile([P, G, P // G], F32, name="share")
        nc.scalar.activation(
            share[:],
            page_exp[:].rearrange("q (g b) -> q g b", b=1).to_broadcast([P, G, P // G]),
            ACT.Copy,
            scale=inv_sum[:],
        )
        share_t = ps.tile([P, Q], F32, name="share_t")
        nc.tensor.transpose(share_t[:], share[:].rearrange("q g b -> q (g b)"), ident[:])
        gate_t = ps.tile([P, PACK, Q], F32, name="gate_t")
        for t in range(PACK):
            nc.tensor.transpose(gate_t[:, t, :], gate[:, t, :], ident[:])
        gate_os = sb.tile([P, PACK, Q], F32, name="gate_os", tag="slot_e", align_bytes=64)
        for t in range(PACK):
            nc.scalar.activation(gate_os[:, t, :], gate_t[:, t, :], ACT.Copy, scale=os_cols[:, t : t + 1])
        first_bf = sb.tile([P, 2 * I], BF16, name="first_bf", tag="slot_d", align_bytes=64)
        last_bf = sb.tile([P, P * PACK], BF16, name="last_bf", align_bytes=64)
        for j in range(E_TILES):
            val_pool = sb.tile([P, T], F32, name="val_pool%d" % j, tag=VAL_SLOTS[j], align_bytes=64)
            nc.sync.dma_start(out=val_pool[:], in_=vals[j * P : (j + 1) * P, :])
            picked = sb.tile([P, I], BF16, name="picked%d" % j, tag=PICK_SLOTS[j], align_bytes=64)
            nc.vector.tensor_copy(picked[:], val_pool[:].indirect(offsets[:]))
            pairs = picked[:].bitcast(F32)
            turned = ps.tile([P, 2, P], F32, name="turned", bufs=2)
            for u in range(2):
                nc.tensor.transpose(turned[:, u, :], pairs[:, u : I // 2 : 2], ident[:])
            if j == 2:
                mixed_bf = sb.tile([P, 2 * I], BF16, name="mixed_bf", tag="slot_b", align_bytes=64)
                nc.vector.tensor_tensor(
                    mixed_bf[:, :I].rearrange("p (q t) -> p q t", t=PACK),
                    gate_os[:].rearrange("p t q -> p q t"),
                    share_t[:].rearrange("p (q a) -> p q a", a=1).to_broadcast([P, Q, PACK]),
                    ALU.mult,
                )
                vals_bf = mixed_bf[:, I:]
            elif j == 3:
                vals_bf = last_bf[:]
            else:
                vals_bf = first_bf[:, j * I : (j + 1) * I]
            copy_out = nc.vector.tensor_copy if j == 3 else nc.scalar.copy
            copy_out(
                vals_bf.bitcast(F32).rearrange("p (e u) -> p e u", u=2), turned[:].rearrange("p u e -> p e u")
            )

        early_codes = sb.tile([P, E_TILES * P], U32, name="early_codes", tag="slot_c", align_bytes=64)
        early_scales = sb.tile([P, E_TILES * P], U8, name="early_scales", align_bytes=64)
        nc.vector.quantize_mx(
            out=early_codes[:, : 2 * P].bitcast(FP8X4), scales=early_scales[:, : 2 * P], in_=mixed_bf[:]
        )
        nc.vector.quantize_mx(
            out=early_codes[:, 2 * P :].bitcast(FP8X4), scales=early_scales[:, 2 * P :], in_=first_bf[:]
        )
        last_codes = sb.tile([P, P], U32, name="last_codes", align_bytes=64)
        last_scales = sb.tile([P, P], U8, name="last_scales", align_bytes=64)
        nc.vector.quantize_mx(out=last_codes[:].bitcast(FP8X4), scales=last_scales[:], in_=last_bf[:])

        acc_early = ps.tile([Q, E - P], F32, name="acc_early")
        acc_last = ps.tile([Q, P], F32, name="acc_last")
        for acc, codes, scales in (
            (acc_early[:, 2 * P :], early_codes[:, Q : Q + P], early_scales[:, Q : Q + P]),
            (acc_early[:, : 2 * P], early_codes[:, Q + P :], early_scales[:, Q + P :]),
            (acc_last[:], last_codes[:], last_scales[:]),
        ):
            nc.tensor.matmul_mx(
                out=acc,
                lhsT=early_codes[:, :Q].bitcast(FP8X4),
                lhsT_scale=early_scales[:, :Q],
                rhs=codes.bitcast(FP8X4),
                rhs_scale=scales,
                start=True,
                stop=True,
            )
        result_early = sb.tile([Q, E - P], F32, name="result_early")
        nc.scalar.copy(result_early[:], acc_early[:])
        nc.sync.dma_start(out=out[:, : E - P], in_=result_early[:])
        result_last = sb.tile([Q, P], F32, name="result_last")
        nc.scalar.copy(result_last[:], acc_last[:])
        nc.scalar.dma_start(out=out[:, E - P :], in_=result_last[:])
